import numpy as np
import ml_dtypes


def mxq(x, axis, fmt="e4m3"):
    dtype, down = {"e4m3": (ml_dtypes.float8_e4m3fn, 7), "e5m2": (ml_dtypes.float8_e5m2, 14)}[fmt]
    v = np.moveaxis(np.asarray(x, np.float32).astype(ml_dtypes.bfloat16).astype(np.float64), axis, -1)
    blocks = v.reshape(v.shape[:-1] + (-1, 32))
    amax = np.abs(blocks).max(-1, keepdims=True)
    byte = np.maximum(np.where(amax > 0, np.frexp(amax)[1] - 1 + 127, 0) - down, 1)
    scale = np.exp2(byte - 127.0)
    codes = (blocks / scale).astype(np.float32).astype(dtype).astype(np.float64)
    return np.moveaxis((codes * scale).reshape(v.shape), -1, axis)


WIDE = False


def mx_kscale(k):
    if not WIDE:
        return np.ones(k)
    levels = np.array([10, -10, 5, -5, 0])
    if k % 512:
        return np.exp2(np.random.permutation(np.resize(levels, k // 32))).repeat(32)
    a = np.empty((k // 512, 16))
    for p in range(k // 512):
        a[p, :8] = np.random.permutation(np.resize(levels, 8))
        for g in range(8):
            far = levels[np.abs(levels - a[p, g]) >= 10]
            a[p, g + 8] = far[np.random.randint(len(far))]
    return np.exp2(a.ravel()).repeat(32)


BF16 = ml_dtypes.bfloat16


def bf(x):
    return np.asarray(x, np.float32).astype(BF16)


def f64(x):
    return np.asarray(x).astype(np.float64)

def planes(Y):
    n, m = Y.shape
    b = f64(bf(Y)).reshape(n // 32, 32, m)
    amax = np.abs(b).max(1)
    byte = np.clip(np.where(amax > 0, np.frexp(amax)[1] - 1 + 127 - 7, 1), 1, 254)
    codes = (b * np.exp2(127.0 - byte)[:, None, :]).reshape(n, m).astype(np.float32).astype(ml_dtypes.float8_e4m3fn).view(np.uint8)
    words = codes.reshape(n // 512, 128, 4, m).transpose(0, 1, 3, 2)
    return np.ascontiguousarray(words), np.ascontiguousarray(byte.astype(np.uint8).reshape(n // 512, 16, m))


B, S, C, H = 4, 1024, 768, 1024
GELU_C = np.sqrt(2.0 / np.pi)


def setup_inputs():
    s = mx_kscale(S)
    patches = np.random.randn(B, S, C) * s[None, :, None]
    w_mix = np.random.randn(H, S) / np.sqrt(S) / s[None, :]
    row_bias = 0.4 * np.random.randn(H)
    row_scale = np.exp(0.8 * np.random.randn(H))
    return {
        "patches": bf(patches),
        "w_mix": bf(w_mix),
        "row_bias": bf(row_bias),
        "row_scale": bf(row_scale),
    }


def reference(patches, w_mix, row_bias, row_scale):
    x = f64(patches).transpose(1, 0, 2).reshape(S, B * C)
    xq = mxq(x, 0, "e4m3")
    wq = mxq(f64(w_mix), 1, "e4m3")
    z = (wq @ xq) + f64(row_bias)[:, None]
    a = 0.5 * z * (1.0 + np.tanh(GELU_C * (z + 0.044715 * z * z * z)))
    h = a * f64(row_scale)[:, None]
    y = h.T.reshape(B, C, H)
    Y = y.reshape(B * C, H).T
    words, scales = planes(Y)
    return y, words, scales

@@ -1,0 +1,286 @@
+from contextlib import ExitStack
+
+import concourse.mybir as mybir
+from concourse.masks import make_identity
+
+B, S, C, H = 4, 1024, 768, 1024
+M = B * C
+FLOPS = 2 * H * S * M
+
+F32 = mybir.dt.float32
+BF16 = mybir.dt.bfloat16
+I32 = mybir.dt.int32
+U32 = mybir.dt.uint32
+U8 = mybir.dt.uint8
+FP8X4 = mybir.dt.float8_e4m3fn_x4
+GELU = mybir.ActivationFunctionType.Gelu_apprx_tanh
+MULT = mybir.AluOpType.mult
+
+P = 128
+PACK = 4
+GROUP = P * PACK
+PASSES = S // GROUP
+HGROUPS = H // GROUP
+CHUNK = 512
+CHUNKS = M // CHUNK
+UNITS = CHUNKS * HGROUPS
+HALVES = 2 * UNITS
+X_AHEAD = 3
+VECTOR_BANKS = {(19, 1), (20, 1), (21, 1), (22, 1), (23, 1)}
+SCALE_STORES = {9: (0, 5), 11: (5, 6)}
+
+
+def chunk_segments(n):
+    segments = []
+    m = n * CHUNK
+    while m < (n + 1) * CHUNK:
+        b, c = divmod(m, C)
+        width = min(C - c, (n + 1) * CHUNK - m)
+        segments.append((b, c, width, m - n * CHUNK))
+        m += width
+    return segments
+
+
+def interleave(engine_copy, dst, src):
+    engine_copy(
+        out=dst.rearrange("p (c i) t -> p c t i", i=4),
+        in_=src.rearrange("p t (c i) -> p c t i", i=4),
+    )
+
+
+def tile_token_mixing_hidden_planes_g1_kernel(tc, patches, w_mix, row_bias, row_scale, out_0, out_1, out_2):
+    nc = tc.nc
+    y_rows = out_0.rearrange("b c h -> (b c) h")
+    y_words = out_1.rearrange("g p m t -> g p (m t)").bitcast(I32)
+    y_scales = out_2.bitcast(I32)
+
+    with ExitStack() as ctx:
+        keep = ctx.enter_context(tc.tile_pool(name="keep", bufs=1))
+        work = ctx.enter_context(tc.tile_pool(name="work", bufs=3))
+        psum = ctx.enter_context(tc.psum_pool(name="psum", bufs=4))
+        ctx.enter_context(tc.manual_schedule())
+
+        ident = keep.tile([P, P], F32, name="ident")
+        make_identity(nc, ident[:])
+        bias = keep.tile([P, HGROUPS, PACK], BF16, name="bias")
+        gain = keep.tile([P, HGROUPS, PACK], BF16, name="gain")
+        nc.scalar.dma_start(out=bias[:], in_=row_bias.rearrange("(g p t) -> p g t", p=P, t=PACK))
+        nc.scalar.dma_start(out=gain[:], in_=row_scale.rearrange("(g p t) -> p g t", p=P, t=PACK))
+        warm = keep.tile([P, 1], F32, name="warm")
+        nc.scalar.activation(out=warm[:], in_=ident[:, 0:1], func=GELU)
+
+        w_raw, x_raw = {}, {}
+        for q in range(2 * HGROUPS):
+            w_raw[q] = keep.tile([P, 2, S], BF16, name="w_raw%d" % q)
+        for b in range(B):
+            for j in range(PASSES):
+                x_raw[b, j] = keep.tile([P, PACK, C], BF16, name="x_raw%d_%d" % (b, j))
+
+        def load_w(q):
+            g, pair = divmod(q, 2)
+            rows = w_mix[g * GROUP : (g + 1) * GROUP, :].rearrange("(p t) k -> p t k", t=PACK)
+            nc.sync.dma_start(out=w_raw[q][:], in_=rows[:, 2 * pair : 2 * pair + 2, :])
+
+        def load_x(b, j, c0, c1):
+            rows = patches[b, j * GROUP : (j + 1) * GROUP, :].rearrange("(p t) c -> p t c", t=PACK)
+            nc.sync.dma_start(out=x_raw[b, j][:, :, c0:c1], in_=rows[:, :, c0:c1])
+
+        load_w(0)
+        load_x(0, 0, 0, CHUNK)
+        load_x(0, 1, 0, CHUNK)
+        for q in range(1, 2 * HGROUPS):
+            load_w(q)
+        for j in range(PASSES):
+            load_x(0, j, CHUNK, C)
+            load_x(1, j, 0, C)
+        for b in range(2, B):
+            for j in range(PASSES):
+                load_x(b, j, 0, C)
+
+        w_banks, w_grouped, w_codes, w_scales = {}, {}, {}, {}
+
+        def w_turn(q):
+            words = w_raw[q][:].bitcast(F32)
+            for j in range(PASSES):
+                bank = psum.tile([P, 2, 2, P], F32, name="turn", tag="turn")
+                w_banks[q, j] = bank
+                for a in range(2):
+                    for u in range(2):
+                        nc.tensor.transpose(bank[:, a, u, :], words[:, a, 2 * P * j + u : 2 * P * (j + 1) : 2], ident[:])
+
+        def w_empty(q):
+            grouped = work.tile([P, PASSES, 2, P, 2], F32, name="w_grouped", tag="w_grouped", bufs=2, align_bytes=64)
+            w_grouped[q] = grouped
+            for j in range(PASSES):
+                nc.scalar.copy(out=grouped[:, j], in_=w_banks[q, j][:].rearrange("p a u r -> p a r u"))
+
+        def w_quantize(q):
+            w_codes[q] = keep.tile([P, PASSES, 2, P], U32, name="w_codes%d" % q, align_bytes=64)
+            w_scales[q] = keep.tile([P, PASSES, 2, P], U8, name="w_scales%d" % q, align_bytes=64)
+            nc.vector.quantize_mx(
+                out=w_codes[q][:].rearrange("p j a r -> p (j a r)").bitcast(FP8X4),
+                scales=w_scales[q][:].rearrange("p j a r -> p (j a r)"),
+                in_=w_grouped[q][:].rearrange("p j a r u -> p (j a r u)").bitcast(BF16),
+            )
+
+        x_grouped, x_codes, x_scales = {}, {}, {}
+
+        def x_interleave(x):
+            n, j = divmod(x, PASSES)
+            grouped = work.tile([P, CHUNK, PACK], BF16, name="x_grouped", tag="x_grouped", align_bytes=64)
+            x_grouped[x] = grouped
+            for b, c, width, at in chunk_segments(n):
+                interleave(nc.vector.tensor_copy, grouped[:, at : at + width, :], x_raw[b, j][:, :, c : c + width])
+
+        def x_quantize(x):
+            x_codes[x] = keep.tile([P, CHUNK], U32, name="x_codes%d" % x, align_bytes=64)
+            x_scales[x] = keep.tile([P, CHUNK], U8, name="x_scales%d" % x, align_bytes=64)
+            nc.vector.quantize_mx(
+                out=x_codes[x][:].bitcast(FP8X4),
+                scales=x_scales[x][:],
+                in_=x_grouped[x][:].rearrange("p m t -> p (m t)"),
+            )
+
+        sums, gelus, scaled, turned, y_grouped = {}, {}, {}, {}, {}
+        out_scales = keep.tile([P, HGROUPS, M], U8, name="out_scales", align_bytes=64)
+
+        def multiply(half):
+            unit, pair = divmod(half, 2)
+            n, g = divmod(unit, HGROUPS)
+            q = 2 * g + pair
+            for a in range(2):
+                bank = psum.tile([P, CHUNK], F32, name="sums", tag="sums")
+                sums[half, a] = bank
+                for j in range(PASSES):
+                    x = PASSES * n + j
+                    nc.tensor.matmul_mx(
+                        out=bank[:],
+                        lhsT=w_codes[q][:, j, a, :].bitcast(FP8X4),
+                        lhsT_scale=w_scales[q][:, j, a, :],
+                        rhs=x_codes[x][:].bitcast(FP8X4),
+                        rhs_scale=x_scales[x][:],
+                        start=(j == 0),
+                        stop=(j == PASSES - 1),
+                    )
+
+        def gelu(half):
+            unit, pair = divmod(half, 2)
+            g = unit % HGROUPS
+            for a in range(2):
+                t = 2 * pair + a
+                act = work.tile([P, CHUNK], F32, name="act", tag="act", bufs=6)
+                gelus[half, a] = act
+                nc.scalar.activation(out=act[:], in_=sums[half, a][:], func=GELU, bias=bias[:, g, t : t + 1])
+
+        def scale(half):
+            unit, pair = divmod(half, 2)
+            g = unit % HGROUPS
+            if pair == 0:
+                scaled[unit] = work.tile([P, PACK, CHUNK], F32, name="scaled", tag="scaled")
+            for a in range(2):
+                t = 2 * pair + a
+                nc.vector.tensor_scalar(
+                    out=scaled[unit][:, t, :], in0=gelus[half, a][:], scalar1=gain[:, g, t : t + 1], scalar2=None, op0=MULT
+                )
+
+        def turn(half):
+            unit, pair = divmod(half, 2)
+            for a in range(2):
+                block = 2 * pair + a
+                bank = psum.tile([P, PACK, P], F32, name="turn", tag="turn")
+                turned[half, a] = bank
+                for t in range(PACK):
+                    nc.tensor.transpose(bank[:, t, :], scaled[unit][:, t, block * P : (block + 1) * P], ident[:])
+
+        rows_out = {}
+
+        def empty(half, a, copy):
+            if half not in rows_out:
+                rows_out[half] = work.tile([P, 2, P, PACK], F32, name="rows_out", tag="rows_out", bufs=5)
+            copy(out=rows_out[half][:, a], in_=turned[half, a][:].rearrange("m t p -> m p t"))
+
+        def store_rows(half):
+            unit, pair = divmod(half, 2)
+            n, g = divmod(unit, HGROUPS)
+            m0 = n * CHUNK + 2 * P * pair
+            nc.sync.dma_start(
+                out=y_rows[m0 : m0 + 2 * P, g * GROUP : (g + 1) * GROUP].rearrange("(a m) h -> m a h", a=2),
+                in_=rows_out[half][:].rearrange("m a p t -> m a (p t)"),
+            )
+
+        def y_interleave(unit):
+            grouped = work.tile([P, CHUNK, PACK], BF16, name="y_grouped", tag="y_grouped", bufs=2, align_bytes=64)
+            y_grouped[unit] = grouped
+            interleave(nc.vector.tensor_copy, grouped[:], scaled[unit][:])
+
+        def y_quantize(unit):
+            n, g = divmod(unit, HGROUPS)
+            cols = slice(n * CHUNK, (n + 1) * CHUNK)
+            codes = work.tile([P, CHUNK], U32, name="y_codes", tag="y_codes", align_bytes=64)
+            nc.vector.quantize_mx(
+                out=codes[:].bitcast(FP8X4),
+                scales=out_scales[:, g, cols],
+                in_=y_grouped[unit][:].rearrange("p m t -> p (m t)"),
+            )
+            nc.sync.dma_start(out=y_words[g, :, cols], in_=codes[:].bitcast(I32))
+            if unit in SCALE_STORES:
+                n0, n1 = SCALE_STORES[unit]
+                for quad in range(4):
+                    nc.sync.dma_start(
+                        out=y_scales[:, 4 * quad : 4 * quad + 4, n0 * CHUNK // 4 : n1 * CHUNK // 4].rearrange("g r w -> r g w"),
+                        in_=out_scales[32 * quad : 32 * quad + 4, :, n0 * CHUNK : n1 * CHUNK].bitcast(I32),
+                    )
+
+        w_turn(0)
+        w_empty(0)
+        x_interleave(0)
+        x_interleave(1)
+        w_quantize(0)
+        x_quantize(0)
+        x_quantize(1)
+        w_turn(1)
+        w_empty(1)
+        w_quantize(1)
+        w_turn(2)
+        w_empty(2)
+        multiply(0)
+        w_quantize(2)
+        w_turn(3)
+
+        for step in range(HALVES + 2):
+            unit, pair = divmod(step, 2)
+            back = step - 2
+            if step + 1 < HALVES:
+                multiply(step + 1)
+            if back >= 0:
+                turn(back)
+            if step < HALVES:
+                gelu(step)
+            if step == 0:
+                w_empty(3)
+                x_interleave(2)
+                w_quantize(3)
+                x_quantize(2)
+            if back >= 0:
+                for a in range(2):
+                    if (back, a) not in VECTOR_BANKS:
+                        empty(back, a, nc.scalar.copy)
+            if step < HALVES:
+                scale(step)
+            x = unit + X_AHEAD
+            if pair == 0:
+                if x < PASSES * CHUNKS:
+                    x_interleave(x)
+            else:
+                if x < PASSES * CHUNKS:
+                    x_quantize(x)
+            if back >= 0:
+                for a in range(2):
+                    if (back, a) in VECTOR_BANKS:
+                        empty(back, a, nc.vector.tensor_copy)
+                store_rows(back)
+            if pair == 0:
+                if unit >= 1:
+                    y_quantize(unit - 1)
+            elif unit < UNITS:
+                y_interleave(unit)

@@ -21,24 +21,16 @@ PACK = 4
 GROUP = P * PACK
 PASSES = S // GROUP
 HGROUPS = H // GROUP
-CHUNK = 512
-CHUNKS = M // CHUNK
+WIDTHS = [256,512,512,512,512,512,256]
+STARTS = [sum(WIDTHS[:n]) for n in range(len(WIDTHS) + 1)]
+CHUNKS = len(WIDTHS)
 UNITS = CHUNKS * HGROUPS
-HALVES = 2 * UNITS
-X_AHEAD = 3
-VECTOR_BANKS = {(19, 1), (20, 1), (21, 1), (22, 1), (23, 1)}
-SCALE_STORES = {9: (0, 5), 11: (5, 6)}
-
-
-def chunk_segments(n):
-    segments = []
-    m = n * CHUNK
-    while m < (n + 1) * CHUNK:
-        b, c = divmod(m, C)
-        width = min(C - c, (n + 1) * CHUNK - m)
-        segments.append((b, c, width, m - n * CHUNK))
-        m += width
-    return segments
+LOADS = [("w",0),("x",0,0,0,768),("w",1),("w",2),("x",0,1,0,768),("w",3),("w",4),("x",1,1,0,768),("w",5),("x",1,0,0,768),("w",6),("w",7),("x",2,0,0,768),("x",2,1,0,768),("x",3,0,0,768),("x",3,1,0,768)]
+X_PIECES = {2: [256,256], 3: [256,256], 6: [64,448], 7: [64,448], 8: [64,448], 9: [64,448], 10: [64,448], 11: [64,448]}
+STORE_BLOCKS = {12: 1, 13: 1}
+FLIPPED = "xi2.0 xi3.0 xi6.0 xi8.0 xi9.0 xi10.0 xi11.0 we0 em3.0 em9.0 em10.0 em10.3 em11.2 em13.1".split()
+ORDER = """wt0 wt1 wt2 wt3 xi2.0 we1 we2 we0 xi0.0 xi2.1 xq0 xq2 wq0 wq1 xi1.0 xi3.1 xq1 wq2 wt4 mm0 mm1 xi3.0 we3 we4 ge0 ge1 xq3 wq3 xi5.0 wq4 sc0 xq5 xi4.0 sc1 mm9 mm2 mm3 wt5 mm8 wt6 wt7 ge9 ge2 xi6.0 we5 ge3 ge8 we6 we7 wq5 xq4 sc2 sc3 sc8 wq6 sc9 yi0 mm10 mm11 mm5 tu0.0 mm6 ge10 ge11 ge5 em0.0 ge6 sc10 yq0 sc11 wq7 yi2 sc5 sc6 xi6.1 yq2 yd0 mm12 mm13 mm18 mm4 tu0.1 ge12 ge13 ge18 ge4 em0.1 st0.0 mm7 tu2.0 tu2.1 tu2.2 tu2.3 mm14 mm15 mm16 ge7 em2.0 em2.1 em2.2 ge14 sc7 sc18 sc4 xi7.0 sc12 yi1 sc13 xq6 sc14 yq1 st2.0 yd2 tu1.0 mm17 mm19 tu1.1 ge15 em2.3 ge16 ge17 em1.0 ge19 em1.1 sc15 xi7.1 sc16 sc17 st2.1 yd1 st1.0 tu3.0 tu3.1 mm20 mm21 tu3.2 tu3.3 mm22 mm23 em3.1 ge20 ge21 xi8.0 em3.2 em3.3 ge22 ge23 em3.0 sc19 yi3 xq7 sc20 sc21 xi8.1 yq3 sc22 sc23 yi4 xq8 st3.0 yd3 st3.1 tu4.0 tu4.1 mm24 mm25 tu4.2 tu4.3 mm26 mm27 em4.0 em4.1 ge24 ge25 xi9.0 em4.2 em4.3 ge26 ge27 sc24 sc25 xi9.1 yq4 sc26 sc27 yi5 xq9 st4.0 yd4 st4.1 tu5.0 tu5.1 mm28 mm29 tu5.2 tu5.3 mm30 mm31 em5.0 em5.1 ge28 ge29 xi10.0 em5.2 em5.3 ge30 ge31 sc28 sc29 xi10.1 yq5 sc30 sc31 yi6 xq10 st5.0 yd5 st5.1 tu6.0 tu6.1 mm32 mm33 tu6.2 tu6.3 mm34 mm35 em6.0 em6.1 ge32 ge33 xi11.0 em6.2 em6.3 ge34 ge35 sc32 sc33 xi11.1 yq6 sc34 sc35 yi7 xq11 st6.0 yd6 st6.1 tu7.0 tu7.1 mm36 mm37 tu7.2 tu7.3 mm38 mm39 em7.0 em7.1 ge36 ge37 em7.2 em7.3 ge38 ge39 sc36 sc37 xi12.0 yq7 yi8 sc38 yq8 sc39 st7.0 st7.1 yd7 tu8.0 tu8.1 mm40 tu8.2 mm41 mm42 tu8.3 mm43 em8.0 ge40 em8.1 em8.2 ge41 em8.3 ge42 ge43 sc40 yi9 sc41 yq9 sc42 st8.0 yd8 st8.1 sd9 yd9 mm44 tu9.0 tu9.1 tu9.2 mm45 tu9.3 mm46 em9.1 ge44 em9.2 ge45 ge46 em9.3 em9.0 sc43 xi13.0 xq12 sc44 xq13 sc45 st9.0 st9.1 tu10.0 tu10.1 tu10.2 mm47 mm48 tu10.3 mm49 mm50 em10.1 ge47 ge48 em10.2 ge49 ge50 em10.0 yi10 sc46 sc47 yq10 em10.3 sc48 sc49 sc50 st10.0 yd10 st10.1 mm51 mm52 tu11.0 tu11.1 tu11.2 tu11.3 mm53 ge51 em11.0 em11.1 em11.3 ge52 ge53 sc51 yi11 em11.2 yi12 sc52 sc53 st11.0 st11.1 tu12.0 mm54 mm55 tu12.1 ge54 ge55 em12.0 em12.1 sc54 sc55 yq11 yq12 yi13 yq13 st12.0 yd11 yd12 st12.1 tu13.0 tu13.1 em13.0 em13.1 st13.0 st13.1 yd13 sd13""".split()
+SCALE_STORES = {9: (0,5), 13: (5,7)}
 
 
 def interleave(engine_copy, dst, src):
@@ -56,231 +48,198 @@ def tile_token_mixing_hidden_planes_g1_kernel(tc, patches, w_mix, row_bias, row_
 
     with ExitStack() as ctx:
         keep = ctx.enter_context(tc.tile_pool(name="keep", bufs=1))
-        work = ctx.enter_context(tc.tile_pool(name="work", bufs=3))
-        psum = ctx.enter_context(tc.psum_pool(name="psum", bufs=4))
+        work = ctx.enter_context(tc.tile_pool(name="work", bufs=1))
+        psum = ctx.enter_context(tc.psum_pool(name="psum", bufs=1))
         ctx.enter_context(tc.manual_schedule())
 
         ident = keep.tile([P, P], F32, name="ident")
         make_identity(nc, ident[:])
-        bias = keep.tile([P, HGROUPS, PACK], BF16, name="bias")
-        gain = keep.tile([P, HGROUPS, PACK], BF16, name="gain")
-        nc.scalar.dma_start(out=bias[:], in_=row_bias.rearrange("(g p t) -> p g t", p=P, t=PACK))
-        nc.scalar.dma_start(out=gain[:], in_=row_scale.rearrange("(g p t) -> p g t", p=P, t=PACK))
+        rows16 = [keep.tile([P, HGROUPS, PACK], BF16, name="rows16_%d" % k) for k in range(2)]
+        rows32 = keep.tile([P, 2, HGROUPS, PACK], F32, name="rows32")
+        bias, gain = rows32[:, 0], rows32[:, 1]
         warm = keep.tile([P, 1], F32, name="warm")
         nc.scalar.activation(out=warm[:], in_=ident[:, 0:1], func=GELU)
 
         w_raw, x_raw = {}, {}
-        for q in range(2 * HGROUPS):
-            w_raw[q] = keep.tile([P, 2, S], BF16, name="w_raw%d" % q)
-        for b in range(B):
-            for j in range(PASSES):
-                x_raw[b, j] = keep.tile([P, PACK, C], BF16, name="x_raw%d_%d" % (b, j))
+        for q in range(PACK * HGROUPS):
+            w_raw[q] = keep.tile([P, S], BF16, name="w_raw%d" % q)
 
         def load_w(q):
-            g, pair = divmod(q, 2)
+            g, t = divmod(q, PACK)
             rows = w_mix[g * GROUP : (g + 1) * GROUP, :].rearrange("(p t) k -> p t k", t=PACK)
-            nc.sync.dma_start(out=w_raw[q][:], in_=rows[:, 2 * pair : 2 * pair + 2, :])
+            nc.sync.dma_start(out=w_raw[q][:], in_=rows[:, t, :])
 
         def load_x(b, j, c0, c1):
             rows = patches[b, j * GROUP : (j + 1) * GROUP, :].rearrange("(p t) c -> p t c", t=PACK)
-            nc.sync.dma_start(out=x_raw[b, j][:, :, c0:c1], in_=rows[:, :, c0:c1])
+            x_raw[b, j, c0, c1] = keep.tile([P, PACK, c1 - c0], BF16, name="x_raw%d_%d_%d" % (b, j, c0))
+            nc.sync.dma_start(out=x_raw[b, j, c0, c1][:], in_=rows[:, :, c0:c1])
 
-        load_w(0)
-        load_x(0, 0, 0, CHUNK)
-        load_x(0, 1, 0, CHUNK)
-        for q in range(1, 2 * HGROUPS):
-            load_w(q)
-        for j in range(PASSES):
-            load_x(0, j, CHUNK, C)
-            load_x(1, j, 0, C)
-        for b in range(2, B):
-            for j in range(PASSES):
-                load_x(b, j, 0, C)
+        for place, item in enumerate(LOADS):
+            if item[0] == "w":
+                load_w(item[1])
+            else:
+                load_x(*item[1:])
+            if place == 3:
+                for k, vec in enumerate((row_bias, row_scale)):
+                    nc.sync.dma_start(out=rows16[k][:], in_=vec.rearrange("(g p t) -> p g t", p=P, t=PACK))
+                    nc.gpsimd.tensor_copy(out=rows32[:, k], in_=rows16[k][:])
+
+        counts = {}
+
+        def slot(kind, depth):
+            counts[kind] = counts.get(kind, -1) + 1
+            return "%s%d" % (kind, counts[kind] % depth)
 
         w_banks, w_grouped, w_codes, w_scales = {}, {}, {}, {}
 
         def w_turn(q):
             words = w_raw[q][:].bitcast(F32)
+            bank = psum.tile([P, PASSES, 2, P], F32, name="turn", tag=slot("turn", 4))
+            w_banks[q] = bank
             for j in range(PASSES):
-                bank = psum.tile([P, 2, 2, P], F32, name="turn", tag="turn")
-                w_banks[q, j] = bank
-                for a in range(2):
-                    for u in range(2):
-                        nc.tensor.transpose(bank[:, a, u, :], words[:, a, 2 * P * j + u : 2 * P * (j + 1) : 2], ident[:])
+                for u in range(2):
+                    nc.tensor.transpose(bank[:, j, u, :], words[:, 2 * P * j + u : 2 * P * (j + 1) : 2], ident[:])
 
-        def w_empty(q):
-            grouped = work.tile([P, PASSES, 2, P, 2], F32, name="w_grouped", tag="w_grouped", bufs=2, align_bytes=64)
+        def w_empty(q, copy):
+            grouped = work.tile([P, PASSES, P, 2], F32, name="w_grouped", tag="w_grouped%d" % (q % 3), align_bytes=64)
             w_grouped[q] = grouped
-            for j in range(PASSES):
-                nc.scalar.copy(out=grouped[:, j], in_=w_banks[q, j][:].rearrange("p a u r -> p a r u"))
+            copy(out=grouped[:], in_=w_banks[q][:].rearrange("p j u r -> p j r u"))
 
         def w_quantize(q):
-            w_codes[q] = keep.tile([P, PASSES, 2, P], U32, name="w_codes%d" % q, align_bytes=64)
-            w_scales[q] = keep.tile([P, PASSES, 2, P], U8, name="w_scales%d" % q, align_bytes=64)
+            w_codes[q] = keep.tile([P, PASSES, P], U32, name="w_codes%d" % q, align_bytes=64)
+            w_scales[q] = keep.tile([P, PASSES, P], U8, name="w_scales%d" % q, align_bytes=64)
             nc.vector.quantize_mx(
-                out=w_codes[q][:].rearrange("p j a r -> p (j a r)").bitcast(FP8X4),
-                scales=w_scales[q][:].rearrange("p j a r -> p (j a r)"),
-                in_=w_grouped[q][:].rearrange("p j a r u -> p (j a r u)").bitcast(BF16),
+                out=w_codes[q][:].rearrange("p j r -> p (j r)").bitcast(FP8X4),
+                scales=w_scales[q][:].rearrange("p j r -> p (j r)"),
+                in_=w_grouped[q][:].rearrange("p j r u -> p (j r u)").bitcast(BF16),
             )
 
         x_grouped, x_codes, x_scales = {}, {}, {}
 
-        def x_interleave(x):
+        def x_interleave(x, piece, copy):
             n, j = divmod(x, PASSES)
-            grouped = work.tile([P, CHUNK, PACK], BF16, name="x_grouped", tag="x_grouped", align_bytes=64)
-            x_grouped[x] = grouped
-            for b, c, width, at in chunk_segments(n):
-                interleave(nc.vector.tensor_copy, grouped[:, at : at + width, :], x_raw[b, j][:, :, c : c + width])
+            if x not in x_grouped:
+                x_grouped[x] = work.tile(
+                    [P, WIDTHS[n], PACK], BF16, name="x_grouped", tag="x_grouped%d" % (x % 3), align_bytes=64
+                )
+            widths = X_PIECES.get(x, [WIDTHS[n]])
+            lo = STARTS[n] + sum(widths[:piece])
+            hi = lo + widths[piece]
+            for (b, jj, c0, c1), raw in x_raw.items():
+                m0, m1 = max(lo, b * C + c0), min(hi, b * C + c1)
+                if jj == j and m0 < m1:
+                    first = b * C + c0
+                    interleave(copy, x_grouped[x][:, m0 - STARTS[n] : m1 - STARTS[n], :], raw[:, :, m0 - first : m1 - first])
 
         def x_quantize(x):
-            x_codes[x] = keep.tile([P, CHUNK], U32, name="x_codes%d" % x, align_bytes=64)
-            x_scales[x] = keep.tile([P, CHUNK], U8, name="x_scales%d" % x, align_bytes=64)
+            width = WIDTHS[x // PASSES]
+            x_codes[x] = keep.tile([P, width], U32, name="x_codes%d" % x, align_bytes=64)
+            x_scales[x] = keep.tile([P, width], U8, name="x_scales%d" % x, align_bytes=64)
             nc.vector.quantize_mx(
                 out=x_codes[x][:].bitcast(FP8X4),
                 scales=x_scales[x][:],
                 in_=x_grouped[x][:].rearrange("p m t -> p (m t)"),
             )
 
-        sums, gelus, scaled, turned, y_grouped = {}, {}, {}, {}, {}
+        sums, gelus, scaled, turned, y_grouped, rows_out, y_codes = {}, {}, {}, {}, {}, {}, {}
         out_scales = keep.tile([P, HGROUPS, M], U8, name="out_scales", align_bytes=64)
 
-        def multiply(half):
-            unit, pair = divmod(half, 2)
+        def multiply(row):
+            unit, t = divmod(row, PACK)
             n, g = divmod(unit, HGROUPS)
-            q = 2 * g + pair
-            for a in range(2):
-                bank = psum.tile([P, CHUNK], F32, name="sums", tag="sums")
-                sums[half, a] = bank
-                for j in range(PASSES):
-                    x = PASSES * n + j
-                    nc.tensor.matmul_mx(
-                        out=bank[:],
-                        lhsT=w_codes[q][:, j, a, :].bitcast(FP8X4),
-                        lhsT_scale=w_scales[q][:, j, a, :],
-                        rhs=x_codes[x][:].bitcast(FP8X4),
-                        rhs_scale=x_scales[x][:],
-                        start=(j == 0),
-                        stop=(j == PASSES - 1),
-                    )
-
-        def gelu(half):
-            unit, pair = divmod(half, 2)
-            g = unit % HGROUPS
-            for a in range(2):
-                t = 2 * pair + a
-                act = work.tile([P, CHUNK], F32, name="act", tag="act", bufs=6)
-                gelus[half, a] = act
-                nc.scalar.activation(out=act[:], in_=sums[half, a][:], func=GELU, bias=bias[:, g, t : t + 1])
-
-        def scale(half):
-            unit, pair = divmod(half, 2)
-            g = unit % HGROUPS
-            if pair == 0:
-                scaled[unit] = work.tile([P, PACK, CHUNK], F32, name="scaled", tag="scaled")
-            for a in range(2):
-                t = 2 * pair + a
-                nc.vector.tensor_scalar(
-                    out=scaled[unit][:, t, :], in0=gelus[half, a][:], scalar1=gain[:, g, t : t + 1], scalar2=None, op0=MULT
+            q = PACK * g + t
+            bank = psum.tile([P, WIDTHS[n]], F32, name="sums", tag=slot("sums", 4))
+            sums[row] = bank
+            for j in range(PASSES):
+                x = PASSES * n + j
+                nc.tensor.matmul_mx(
+                    out=bank[:],
+                    lhsT=w_codes[q][:, j, :].bitcast(FP8X4),
+                    lhsT_scale=w_scales[q][:, j, :],
+                    rhs=x_codes[x][:].bitcast(FP8X4),
+                    rhs_scale=x_scales[x][:],
+                    start=(j == 0),
+                    stop=(j == PASSES - 1),
                 )
 
-        def turn(half):
-            unit, pair = divmod(half, 2)
-            for a in range(2):
-                block = 2 * pair + a
-                bank = psum.tile([P, PACK, P], F32, name="turn", tag="turn")
-                turned[half, a] = bank
-                for t in range(PACK):
-                    nc.tensor.transpose(bank[:, t, :], scaled[unit][:, t, block * P : (block + 1) * P], ident[:])
-
-        rows_out = {}
-
-        def empty(half, a, copy):
-            if half not in rows_out:
-                rows_out[half] = work.tile([P, 2, P, PACK], F32, name="rows_out", tag="rows_out", bufs=5)
-            copy(out=rows_out[half][:, a], in_=turned[half, a][:].rearrange("m t p -> m p t"))
-
-        def store_rows(half):
-            unit, pair = divmod(half, 2)
+        def gelu(row):
+            unit, t = divmod(row, PACK)
             n, g = divmod(unit, HGROUPS)
-            m0 = n * CHUNK + 2 * P * pair
+            act = work.tile([P, WIDTHS[n]], F32, name="act", tag=slot("act", 6))
+            gelus[row] = act
+            nc.scalar.activation(out=act[:], in_=sums[row][:], func=GELU, bias=bias[:, g, t : t + 1])
+
+        def scale(row):
+            unit, t = divmod(row, PACK)
+            n, g = divmod(unit, HGROUPS)
+            if unit not in scaled:
+                scaled[unit] = work.tile([P, PACK, WIDTHS[n]], F32, name="scaled", tag="scaled%d" % (unit % 5))
+            nc.vector.tensor_scalar(
+                out=scaled[unit][:, t, :], in0=gelus[row][:], scalar1=gain[:, g, t : t + 1], scalar2=None, op0=MULT
+            )
+
+        def turn(unit, block):
+            bank = psum.tile([P, PACK, P], F32, name="turn", tag=slot("turn", 4))
+            turned[unit, block] = bank
+            for t in range(PACK):
+                nc.tensor.transpose(bank[:, t, :], scaled[unit][:, t, block * P : (block + 1) * P], ident[:])
+
+        stores = [(u, k) for u in range(UNITS) for k in range(WIDTHS[u // HGROUPS] // P // STORE_BLOCKS.get(u, 2))]
+
+        def empty(unit, block, copy):
+            per = STORE_BLOCKS.get(unit, 2)
+            key = (unit, block // per)
+            if key not in rows_out:
+                rows_out[key] = work.tile([P, per, P, PACK], F32, name="rows_out", tag="rows_out%d" % (stores.index(key) % 5))
+            copy(out=rows_out[key][:, block % per], in_=turned[unit, block][:].rearrange("m t p -> m p t"))
+
+        def store_rows(unit, k):
+            n, g = divmod(unit, HGROUPS)
+            rows = STORE_BLOCKS.get(unit, 2) * P
+            m0 = STARTS[n] + rows * k
             nc.sync.dma_start(
-                out=y_rows[m0 : m0 + 2 * P, g * GROUP : (g + 1) * GROUP].rearrange("(a m) h -> m a h", a=2),
-                in_=rows_out[half][:].rearrange("m a p t -> m a (p t)"),
+                out=y_rows[m0 : m0 + rows, g * GROUP : (g + 1) * GROUP].rearrange("(a m) h -> m a h", m=P),
+                in_=rows_out[unit, k][:].rearrange("m a p t -> m a (p t)"),
             )
 
         def y_interleave(unit):
-            grouped = work.tile([P, CHUNK, PACK], BF16, name="y_grouped", tag="y_grouped", bufs=2, align_bytes=64)
+            width = WIDTHS[unit // HGROUPS]
+            grouped = work.tile([P, width, PACK], BF16, name="y_grouped", tag="y_grouped%d" % (unit % 2), align_bytes=64)
             y_grouped[unit] = grouped
             interleave(nc.vector.tensor_copy, grouped[:], scaled[unit][:])
 
         def y_quantize(unit):
             n, g = divmod(unit, HGROUPS)
-            cols = slice(n * CHUNK, (n + 1) * CHUNK)
-            codes = work.tile([P, CHUNK], U32, name="y_codes", tag="y_codes", align_bytes=64)
+            cols = slice(STARTS[n], STARTS[n + 1])
+            codes = work.tile([P, WIDTHS[n]], U32, name="y_codes", tag="y_codes%d" % (unit % 3), align_bytes=64)
             nc.vector.quantize_mx(
                 out=codes[:].bitcast(FP8X4),
                 scales=out_scales[:, g, cols],
                 in_=y_grouped[unit][:].rearrange("p m t -> p (m t)"),
             )
-            nc.sync.dma_start(out=y_words[g, :, cols], in_=codes[:].bitcast(I32))
-            if unit in SCALE_STORES:
-                n0, n1 = SCALE_STORES[unit]
-                for quad in range(4):
-                    nc.sync.dma_start(
-                        out=y_scales[:, 4 * quad : 4 * quad + 4, n0 * CHUNK // 4 : n1 * CHUNK // 4].rearrange("g r w -> r g w"),
-                        in_=out_scales[32 * quad : 32 * quad + 4, :, n0 * CHUNK : n1 * CHUNK].bitcast(I32),
-                    )
+            y_codes[unit] = codes
 
-        w_turn(0)
-        w_empty(0)
-        x_interleave(0)
-        x_interleave(1)
-        w_quantize(0)
-        x_quantize(0)
-        x_quantize(1)
-        w_turn(1)
-        w_empty(1)
-        w_quantize(1)
-        w_turn(2)
-        w_empty(2)
-        multiply(0)
-        w_quantize(2)
-        w_turn(3)
+        def store_words(unit):
+            n, g = divmod(unit, HGROUPS)
+            nc.sync.dma_start(out=y_words[g, :, STARTS[n] : STARTS[n + 1]], in_=y_codes[unit][:].bitcast(I32))
 
-        for step in range(HALVES + 2):
-            unit, pair = divmod(step, 2)
-            back = step - 2
-            if step + 1 < HALVES:
-                multiply(step + 1)
-            if back >= 0:
-                turn(back)
-            if step < HALVES:
-                gelu(step)
-            if step == 0:
-                w_empty(3)
-                x_interleave(2)
-                w_quantize(3)
-                x_quantize(2)
-            if back >= 0:
-                for a in range(2):
-                    if (back, a) not in VECTOR_BANKS:
-                        empty(back, a, nc.scalar.copy)
-            if step < HALVES:
-                scale(step)
-            x = unit + X_AHEAD
-            if pair == 0:
-                if x < PASSES * CHUNKS:
-                    x_interleave(x)
-            else:
-                if x < PASSES * CHUNKS:
-                    x_quantize(x)
-            if back >= 0:
-                for a in range(2):
-                    if (back, a) in VECTOR_BANKS:
-                        empty(back, a, nc.vector.tensor_copy)
-                store_rows(back)
-            if pair == 0:
-                if unit >= 1:
-                    y_quantize(unit - 1)
-            elif unit < UNITS:
-                y_interleave(unit)
+        def store_scales(unit):
+            m0, m1 = STARTS[SCALE_STORES[unit][0]], STARTS[SCALE_STORES[unit][1]]
+            for quad in range(4):
+                nc.sync.dma_start(
+                    out=y_scales[:, 4 * quad : 4 * quad + 4, m0 // 4 : m1 // 4].rearrange("g r w -> r g w"),
+                    in_=out_scales[32 * quad : 32 * quad + 4, :, m0:m1].bitcast(I32),
+                )
+
+        tasks = {
+            "wt": w_turn, "we": w_empty, "wq": w_quantize, "xi": x_interleave, "xq": x_quantize, "mm": multiply,
+            "ge": gelu, "sc": scale, "tu": turn, "em": empty, "st": store_rows, "yi": y_interleave, "yq": y_quantize,
+            "yd": store_words, "sd": store_scales,
+        }
+        for item in ORDER:
+            kind = item[:2]
+            args = [int(a) for a in item[2:].split(".")]
+            if kind in ("we", "em", "xi"):
+                on_vector = (kind == "xi") != (item in FLIPPED)
+                args.append(nc.vector.tensor_copy if on_vector else nc.scalar.copy)
+            tasks[kind](*args)

@@ -14,37 +14,43 @@ U32 = mybir.dt.uint32
 U8 = mybir.dt.uint8
 FP8X4 = mybir.dt.float8_e4m3fn_x4
 GELU = mybir.ActivationFunctionType.Gelu_apprx_tanh
+COPY = mybir.ActivationFunctionType.Copy
 MULT = mybir.AluOpType.mult
 
 P = 128
 PACK = 4
 GROUP = P * PACK
 PASSES = S // GROUP
-HGROUPS = H // GROUP
-WIDTHS = [256,512,512,512,512,512,256]
+H_GROUPS = H // GROUP
+
+NARROW, WIDE = 256, 512
+WIDTHS = [NARROW] + [WIDE] * 5 + [NARROW]
 STARTS = [sum(WIDTHS[:n]) for n in range(len(WIDTHS) + 1)]
-CHUNKS = len(WIDTHS)
-UNITS = CHUNKS * HGROUPS
-LOADS = [("w",0),("x",0,0,0,768),("w",1),("w",2),("x",0,1,0,768),("w",3),("w",4),("x",1,1,0,768),("w",5),("x",1,0,0,768),("w",6),("w",7),("x",2,0,0,768),("x",2,1,0,768),("x",3,0,0,768),("x",3,1,0,768)]
-X_PIECES = {2: [256,256], 3: [256,256], 6: [64,448], 7: [64,448], 8: [64,448], 9: [64,448], 10: [64,448], 11: [64,448]}
-STORE_BLOCKS = {12: 1, 13: 1}
-FLIPPED = "xi2.0 xi3.0 xi6.0 xi8.0 xi9.0 xi10.0 xi11.0 we0 em3.0 em9.0 em10.0 em10.3 em11.2 em13.1".split()
-ORDER = """wt0 wt1 wt2 wt3 xi2.0 we1 we2 we0 xi0.0 xi2.1 xq0 xq2 wq0 wq1 xi1.0 xi3.1 xq1 wq2 wt4 mm0 mm1 xi3.0 we3 we4 ge0 ge1 xq3 wq3 xi5.0 wq4 sc0 xq5 xi4.0 sc1 mm9 mm2 mm3 wt5 mm8 wt6 wt7 ge9 ge2 xi6.0 we5 ge3 ge8 we6 we7 wq5 xq4 sc2 sc3 sc8 wq6 sc9 yi0 mm10 mm11 mm5 tu0.0 mm6 ge10 ge11 ge5 em0.0 ge6 sc10 yq0 sc11 wq7 yi2 sc5 sc6 xi6.1 yq2 yd0 mm12 mm13 mm18 mm4 tu0.1 ge12 ge13 ge18 ge4 em0.1 st0.0 mm7 tu2.0 tu2.1 tu2.2 tu2.3 mm14 mm15 mm16 ge7 em2.0 em2.1 em2.2 ge14 sc7 sc18 sc4 xi7.0 sc12 yi1 sc13 xq6 sc14 yq1 st2.0 yd2 tu1.0 mm17 mm19 tu1.1 ge15 em2.3 ge16 ge17 em1.0 ge19 em1.1 sc15 xi7.1 sc16 sc17 st2.1 yd1 st1.0 tu3.0 tu3.1 mm20 mm21 tu3.2 tu3.3 mm22 mm23 em3.1 ge20 ge21 xi8.0 em3.2 em3.3 ge22 ge23 em3.0 sc19 yi3 xq7 sc20 sc21 xi8.1 yq3 sc22 sc23 yi4 xq8 st3.0 yd3 st3.1 tu4.0 tu4.1 mm24 mm25 tu4.2 tu4.3 mm26 mm27 em4.0 em4.1 ge24 ge25 xi9.0 em4.2 em4.3 ge26 ge27 sc24 sc25 xi9.1 yq4 sc26 sc27 yi5 xq9 st4.0 yd4 st4.1 tu5.0 tu5.1 mm28 mm29 tu5.2 tu5.3 mm30 mm31 em5.0 em5.1 ge28 ge29 xi10.0 em5.2 em5.3 ge30 ge31 sc28 sc29 xi10.1 yq5 sc30 sc31 yi6 xq10 st5.0 yd5 st5.1 tu6.0 tu6.1 mm32 mm33 tu6.2 tu6.3 mm34 mm35 em6.0 em6.1 ge32 ge33 xi11.0 em6.2 em6.3 ge34 ge35 sc32 sc33 xi11.1 yq6 sc34 sc35 yi7 xq11 st6.0 yd6 st6.1 tu7.0 tu7.1 mm36 mm37 tu7.2 tu7.3 mm38 mm39 em7.0 em7.1 ge36 ge37 em7.2 em7.3 ge38 ge39 sc36 sc37 xi12.0 yq7 yi8 sc38 yq8 sc39 st7.0 st7.1 yd7 tu8.0 tu8.1 mm40 tu8.2 mm41 mm42 tu8.3 mm43 em8.0 ge40 em8.1 em8.2 ge41 em8.3 ge42 ge43 sc40 yi9 sc41 yq9 sc42 st8.0 yd8 st8.1 sd9 yd9 mm44 tu9.0 tu9.1 tu9.2 mm45 tu9.3 mm46 em9.1 ge44 em9.2 ge45 ge46 em9.3 em9.0 sc43 xi13.0 xq12 sc44 xq13 sc45 st9.0 st9.1 tu10.0 tu10.1 tu10.2 mm47 mm48 tu10.3 mm49 mm50 em10.1 ge47 ge48 em10.2 ge49 ge50 em10.0 yi10 sc46 sc47 yq10 em10.3 sc48 sc49 sc50 st10.0 yd10 st10.1 mm51 mm52 tu11.0 tu11.1 tu11.2 tu11.3 mm53 ge51 em11.0 em11.1 em11.3 ge52 ge53 sc51 yi11 em11.2 yi12 sc52 sc53 st11.0 st11.1 tu12.0 mm54 mm55 tu12.1 ge54 ge55 em12.0 em12.1 sc54 sc55 yq11 yq12 yi13 yq13 st12.0 yd11 yd12 st12.1 tu13.0 tu13.1 em13.0 em13.1 st13.0 st13.1 yd13 sd13""".split()
-SCALE_STORES = {9: (0,5), 13: (5,7)}
+UNITS = len(WIDTHS) * H_GROUPS
+UNIT_ORDER = [0, 2, 1] + list(range(3, UNITS))
+
+SUM_BANKS, TURN_BANKS = 4, 4
+W_GROUPED_BUFS, X_GROUPED_BUFS, Y_GROUPED_BUFS = 3, 3, 2
+GELU_BUFS, SCALED_BUFS, ROWS_BUFS, Y_WORDS_BUFS = 8, 5, 5, 3
+
+STEADY_FROM = 5
+SCALAR_SCALES = (6, 7)
+VECTOR_EMPTIES = ((11, 0), (11, 2), (13, 1))
 
 
-def interleave(engine_copy, dst, src):
-    engine_copy(
-        out=dst.rearrange("p (c i) t -> p c t i", i=4),
-        in_=src.rearrange("p t (c i) -> p c t i", i=4),
+def interleave(copy, grouped, rows):
+    copy(
+        out=grouped.rearrange("p (c i) t -> p c t i", i=4),
+        in_=rows.rearrange("p t (c i) -> p c t i", i=4),
     )
 
 
 def tile_token_mixing_hidden_planes_g1_kernel(tc, patches, w_mix, row_bias, row_scale, out_0, out_1, out_2):
     nc = tc.nc
+    on_vector, on_scalar = nc.vector.tensor_copy, nc.scalar.copy
     y_rows = out_0.rearrange("b c h -> (b c) h")
     y_words = out_1.rearrange("g p m t -> g p (m t)").bitcast(I32)
-    y_scales = out_2.bitcast(I32)
+    y_scale_rows = out_2.bitcast(I32)
 
     with ExitStack() as ctx:
         keep = ctx.enter_context(tc.tile_pool(name="keep", bufs=1))
@@ -54,56 +60,70 @@ def tile_token_mixing_hidden_planes_g1_kernel(tc, patches, w_mix, row_bias, row_
 
         ident = keep.tile([P, P], F32, name="ident")
         make_identity(nc, ident[:])
-        rows16 = [keep.tile([P, HGROUPS, PACK], BF16, name="rows16_%d" % k) for k in range(2)]
-        rows32 = keep.tile([P, 2, HGROUPS, PACK], F32, name="rows32")
-        bias, gain = rows32[:, 0], rows32[:, 1]
         warm = keep.tile([P, 1], F32, name="warm")
         nc.scalar.activation(out=warm[:], in_=ident[:, 0:1], func=GELU)
 
         w_raw, x_raw = {}, {}
-        for q in range(PACK * HGROUPS):
-            w_raw[q] = keep.tile([P, S], BF16, name="w_raw%d" % q)
 
         def load_w(q):
             g, t = divmod(q, PACK)
             rows = w_mix[g * GROUP : (g + 1) * GROUP, :].rearrange("(p t) k -> p t k", t=PACK)
+            w_raw[q] = keep.tile([P, S], BF16, name="w_raw%d" % q)
             nc.sync.dma_start(out=w_raw[q][:], in_=rows[:, t, :])
 
-        def load_x(b, j, c0, c1):
+        def load_x(b, j):
             rows = patches[b, j * GROUP : (j + 1) * GROUP, :].rearrange("(p t) c -> p t c", t=PACK)
-            x_raw[b, j, c0, c1] = keep.tile([P, PACK, c1 - c0], BF16, name="x_raw%d_%d_%d" % (b, j, c0))
-            nc.sync.dma_start(out=x_raw[b, j, c0, c1][:], in_=rows[:, :, c0:c1])
+            x_raw[b, j] = keep.tile([P, PACK, C], BF16, name="x_raw%d_%d" % (b, j))
+            nc.sync.dma_start(out=x_raw[b, j][:], in_=rows)
 
-        for place, item in enumerate(LOADS):
-            if item[0] == "w":
-                load_w(item[1])
-            else:
-                load_x(*item[1:])
-            if place == 3:
-                for k, vec in enumerate((row_bias, row_scale)):
-                    nc.sync.dma_start(out=rows16[k][:], in_=vec.rearrange("(g p t) -> p g t", p=P, t=PACK))
-                    nc.gpsimd.tensor_copy(out=rows32[:, k], in_=rows16[k][:])
+        def load_per_row(vec, name):
+            narrow = keep.tile([P, H_GROUPS, PACK], BF16, name=name + "_bf16")
+            wide = keep.tile([P, H_GROUPS, PACK], F32, name=name)
+            nc.sync.dma_start(out=narrow[:], in_=vec.rearrange("(g p t) -> p g t", p=P, t=PACK))
+            nc.gpsimd.tensor_copy(out=wide[:], in_=narrow[:])
+            return wide
 
-        counts = {}
+        load_w(0)
+        load_x(0, 0)
+        load_w(1)
+        load_w(2)
+        bias = load_per_row(row_bias, "bias")
+        gain = load_per_row(row_scale, "gain")
+        load_x(0, 1)
+        load_w(3)
+        load_w(4)
+        load_x(1, 0)
+        load_w(5)
+        load_w(6)
+        load_x(1, 1)
+        load_w(7)
+        for b in range(2, B):
+            for j in range(PASSES):
+                load_x(b, j)
 
-        def slot(kind, depth):
-            counts[kind] = counts.get(kind, -1) + 1
-            return "%s%d" % (kind, counts[kind] % depth)
+        banks_taken = {"sums": 0, "turn": 0}
 
-        w_banks, w_grouped, w_codes, w_scales = {}, {}, {}, {}
+        def psum_bank(kind, depth, shape):
+            tag = "%s%d" % (kind, banks_taken[kind] % depth)
+            banks_taken[kind] += 1
+            return psum.tile(shape, F32, name=kind, tag=tag)
+
+        w_turned, w_grouped, w_codes, w_scales = {}, {}, {}, {}
 
         def w_turn(q):
-            words = w_raw[q][:].bitcast(F32)
-            bank = psum.tile([P, PASSES, 2, P], F32, name="turn", tag=slot("turn", 4))
-            w_banks[q] = bank
+            pairs = w_raw[q][:].bitcast(F32)
+            w_turned[q] = psum_bank("turn", TURN_BANKS, [P, PASSES, 2, P])
             for j in range(PASSES):
                 for u in range(2):
-                    nc.tensor.transpose(bank[:, j, u, :], words[:, 2 * P * j + u : 2 * P * (j + 1) : 2], ident[:])
+                    nc.tensor.transpose(
+                        w_turned[q][:, j, u, :], pairs[:, 2 * P * j + u : 2 * P * (j + 1) : 2], ident[:]
+                    )
 
-        def w_empty(q, copy):
-            grouped = work.tile([P, PASSES, P, 2], F32, name="w_grouped", tag="w_grouped%d" % (q % 3), align_bytes=64)
-            w_grouped[q] = grouped
-            copy(out=grouped[:], in_=w_banks[q][:].rearrange("p j u r -> p j r u"))
+        def w_empty(q):
+            w_grouped[q] = work.tile(
+                [P, PASSES, P, 2], F32, name="w_grouped", tag="w_grouped%d" % (q % W_GROUPED_BUFS), align_bytes=64
+            )
+            on_scalar(out=w_grouped[q][:], in_=w_turned[q][:].rearrange("p j u r -> p j r u"))
 
         def w_quantize(q):
             w_codes[q] = keep.tile([P, PASSES, P], U32, name="w_codes%d" % q, align_bytes=64)
@@ -115,21 +135,22 @@ def tile_token_mixing_hidden_planes_g1_kernel(tc, patches, w_mix, row_bias, row_
             )
 
         x_grouped, x_codes, x_scales = {}, {}, {}
+        wide_x = [x for x in range(UNITS) if WIDTHS[x // PASSES] == WIDE]
 
-        def x_interleave(x, piece, copy):
+        def x_interleave(x, copy=on_vector, lo=0, hi=WIDE):
             n, j = divmod(x, PASSES)
             if x not in x_grouped:
-                x_grouped[x] = work.tile(
-                    [P, WIDTHS[n], PACK], BF16, name="x_grouped", tag="x_grouped%d" % (x % 3), align_bytes=64
-                )
-            widths = X_PIECES.get(x, [WIDTHS[n]])
-            lo = STARTS[n] + sum(widths[:piece])
-            hi = lo + widths[piece]
-            for (b, jj, c0, c1), raw in x_raw.items():
-                m0, m1 = max(lo, b * C + c0), min(hi, b * C + c1)
-                if jj == j and m0 < m1:
-                    first = b * C + c0
-                    interleave(copy, x_grouped[x][:, m0 - STARTS[n] : m1 - STARTS[n], :], raw[:, :, m0 - first : m1 - first])
+                tag = "x_grouped%d" % (wide_x.index(x) % X_GROUPED_BUFS) if x in wide_x else "x_narrow%d" % x
+                x_grouped[x] = work.tile([P, WIDTHS[n], PACK], BF16, name="x_grouped", tag=tag, align_bytes=64)
+            for b in range(B):
+                m0 = max(STARTS[n] + lo, b * C)
+                m1 = min(STARTS[n] + hi, STARTS[n + 1], (b + 1) * C)
+                if m0 < m1:
+                    interleave(
+                        copy,
+                        x_grouped[x][:, m0 - STARTS[n] : m1 - STARTS[n], :],
+                        x_raw[b, j][:, :, m0 - b * C : m1 - b * C],
+                    )
 
         def x_quantize(x):
             width = WIDTHS[x // PASSES]
@@ -141,105 +162,262 @@ def tile_token_mixing_hidden_planes_g1_kernel(tc, patches, w_mix, row_bias, row_
                 in_=x_grouped[x][:].rearrange("p m t -> p (m t)"),
             )
 
-        sums, gelus, scaled, turned, y_grouped, rows_out, y_codes = {}, {}, {}, {}, {}, {}, {}
-        out_scales = keep.tile([P, HGROUPS, M], U8, name="out_scales", align_bytes=64)
+        sums, gelus, scaled = {}, {}, {}
 
-        def multiply(row):
-            unit, t = divmod(row, PACK)
-            n, g = divmod(unit, HGROUPS)
-            q = PACK * g + t
-            bank = psum.tile([P, WIDTHS[n]], F32, name="sums", tag=slot("sums", 4))
-            sums[row] = bank
-            for j in range(PASSES):
-                x = PASSES * n + j
-                nc.tensor.matmul_mx(
-                    out=bank[:],
-                    lhsT=w_codes[q][:, j, :].bitcast(FP8X4),
-                    lhsT_scale=w_scales[q][:, j, :],
-                    rhs=x_codes[x][:].bitcast(FP8X4),
-                    rhs_scale=x_scales[x][:],
-                    start=(j == 0),
-                    stop=(j == PASSES - 1),
+        def multiply(unit, slices=range(PACK)):
+            n, g = divmod(unit, H_GROUPS)
+            for t in slices:
+                q = PACK * g + t
+                sums[unit, t] = psum_bank("sums", SUM_BANKS, [P, WIDTHS[n]])
+                for j in range(PASSES):
+                    x = PASSES * n + j
+                    nc.tensor.matmul_mx(
+                        out=sums[unit, t][:],
+                        lhsT=w_codes[q][:, j, :].bitcast(FP8X4),
+                        lhsT_scale=w_scales[q][:, j, :],
+                        rhs=x_codes[x][:].bitcast(FP8X4),
+                        rhs_scale=x_scales[x][:],
+                        start=(j == 0),
+                        stop=(j == PASSES - 1),
+                    )
+
+        def gelu(unit, slices=range(PACK)):
+            n, g = divmod(unit, H_GROUPS)
+            for t in slices:
+                tag = "gelu%d" % ((PACK * UNIT_ORDER.index(unit) + t) % GELU_BUFS)
+                gelus[unit, t] = work.tile([P, WIDTHS[n]], F32, name="gelu", tag=tag)
+                nc.scalar.activation(
+                    out=gelus[unit, t][:], in_=sums[unit, t][:], func=GELU, bias=bias[:, g, t : t + 1]
                 )
 
-        def gelu(row):
-            unit, t = divmod(row, PACK)
-            n, g = divmod(unit, HGROUPS)
-            act = work.tile([P, WIDTHS[n]], F32, name="act", tag=slot("act", 6))
-            gelus[row] = act
-            nc.scalar.activation(out=act[:], in_=sums[row][:], func=GELU, bias=bias[:, g, t : t + 1])
-
-        def scale(row):
-            unit, t = divmod(row, PACK)
-            n, g = divmod(unit, HGROUPS)
+        def scaled_tile(unit):
             if unit not in scaled:
-                scaled[unit] = work.tile([P, PACK, WIDTHS[n]], F32, name="scaled", tag="scaled%d" % (unit % 5))
-            nc.vector.tensor_scalar(
-                out=scaled[unit][:, t, :], in0=gelus[row][:], scalar1=gain[:, g, t : t + 1], scalar2=None, op0=MULT
+                tag = "scaled%d" % (UNIT_ORDER.index(unit) % SCALED_BUFS)
+                scaled[unit] = work.tile([P, PACK, WIDTHS[unit // H_GROUPS]], F32, name="scaled", tag=tag)
+            return scaled[unit]
+
+        def scale(unit, *slices):
+            for t in slices:
+                nc.vector.tensor_scalar(
+                    out=scaled_tile(unit)[:, t, :],
+                    in0=gelus[unit, t][:],
+                    scalar1=gain[:, unit % H_GROUPS, t : t + 1],
+                    scalar2=None,
+                    op0=MULT,
+                )
+
+        def scale_on_scalar(unit, t):
+            nc.scalar.activation(
+                out=scaled_tile(unit)[:, t, :],
+                in_=gelus[unit, t][:],
+                func=COPY,
+                scale=gain[:, unit % H_GROUPS, t : t + 1],
             )
 
-        def turn(unit, block):
-            bank = psum.tile([P, PACK, P], F32, name="turn", tag=slot("turn", 4))
-            turned[unit, block] = bank
-            for t in range(PACK):
-                nc.tensor.transpose(bank[:, t, :], scaled[unit][:, t, block * P : (block + 1) * P], ident[:])
+        turned, rows_out = {}, {}
 
-        stores = [(u, k) for u in range(UNITS) for k in range(WIDTHS[u // HGROUPS] // P // STORE_BLOCKS.get(u, 2))]
+        def blocks(unit):
+            return range(WIDTHS[unit // H_GROUPS] // P)
 
-        def empty(unit, block, copy):
-            per = STORE_BLOCKS.get(unit, 2)
-            key = (unit, block // per)
-            if key not in rows_out:
-                rows_out[key] = work.tile([P, per, P, PACK], F32, name="rows_out", tag="rows_out%d" % (stores.index(key) % 5))
-            copy(out=rows_out[key][:, block % per], in_=turned[unit, block][:].rearrange("m t p -> m p t"))
+        def blocks_per_store(unit):
+            return 1 if unit >= UNITS - H_GROUPS else 2
+
+        row_stores = [(u, k) for u in UNIT_ORDER for k in range(len(blocks(u)) // blocks_per_store(u))]
+
+        def turn(unit, which):
+            for block in which:
+                turned[unit, block] = psum_bank("turn", TURN_BANKS, [P, PACK, P])
+                for t in range(PACK):
+                    nc.tensor.transpose(
+                        turned[unit, block][:, t, :], scaled[unit][:, t, block * P : (block + 1) * P], ident[:]
+                    )
+
+        def empty(unit, which, copy=on_scalar):
+            per = blocks_per_store(unit)
+            for block in which:
+                key = (unit, block // per)
+                if key not in rows_out:
+                    tag = "rows_out%d" % (row_stores.index(key) % ROWS_BUFS)
+                    rows_out[key] = work.tile([P, per, P, PACK], F32, name="rows_out", tag=tag)
+                copy(out=rows_out[key][:, block % per], in_=turned[unit, block][:].rearrange("m t p -> m p t"))
 
         def store_rows(unit, k):
-            n, g = divmod(unit, HGROUPS)
-            rows = STORE_BLOCKS.get(unit, 2) * P
+            n, g = divmod(unit, H_GROUPS)
+            rows = blocks_per_store(unit) * P
             m0 = STARTS[n] + rows * k
             nc.sync.dma_start(
                 out=y_rows[m0 : m0 + rows, g * GROUP : (g + 1) * GROUP].rearrange("(a m) h -> m a h", m=P),
                 in_=rows_out[unit, k][:].rearrange("m a p t -> m a (p t)"),
             )
 
+        y_grouped, y_codes = {}, {}
+        y_scales = keep.tile([P, H_GROUPS, M], U8, name="y_scales", align_bytes=64)
+
         def y_interleave(unit):
-            width = WIDTHS[unit // HGROUPS]
-            grouped = work.tile([P, width, PACK], BF16, name="y_grouped", tag="y_grouped%d" % (unit % 2), align_bytes=64)
-            y_grouped[unit] = grouped
-            interleave(nc.vector.tensor_copy, grouped[:], scaled[unit][:])
+            tag = "y_grouped%d" % (UNIT_ORDER.index(unit) % Y_GROUPED_BUFS)
+            y_grouped[unit] = work.tile(
+                [P, WIDTHS[unit // H_GROUPS], PACK], BF16, name="y_grouped", tag=tag, align_bytes=64
+            )
+            interleave(on_vector, y_grouped[unit][:], scaled[unit][:])
 
         def y_quantize(unit):
-            n, g = divmod(unit, HGROUPS)
-            cols = slice(STARTS[n], STARTS[n + 1])
-            codes = work.tile([P, WIDTHS[n]], U32, name="y_codes", tag="y_codes%d" % (unit % 3), align_bytes=64)
+            n, g = divmod(unit, H_GROUPS)
+            tag = "y_codes%d" % (UNIT_ORDER.index(unit) % Y_WORDS_BUFS)
+            y_codes[unit] = work.tile([P, WIDTHS[n]], U32, name="y_codes", tag=tag, align_bytes=64)
             nc.vector.quantize_mx(
-                out=codes[:].bitcast(FP8X4),
-                scales=out_scales[:, g, cols],
+                out=y_codes[unit][:].bitcast(FP8X4),
+                scales=y_scales[:, g, STARTS[n] : STARTS[n + 1]],
                 in_=y_grouped[unit][:].rearrange("p m t -> p (m t)"),
             )
-            y_codes[unit] = codes
 
         def store_words(unit):
-            n, g = divmod(unit, HGROUPS)
+            n, g = divmod(unit, H_GROUPS)
             nc.sync.dma_start(out=y_words[g, :, STARTS[n] : STARTS[n + 1]], in_=y_codes[unit][:].bitcast(I32))
 
-        def store_scales(unit):
-            m0, m1 = STARTS[SCALE_STORES[unit][0]], STARTS[SCALE_STORES[unit][1]]
+        def store_scales(first_chunk, end_chunk):
+            m0, m1 = STARTS[first_chunk], STARTS[end_chunk]
             for quad in range(4):
                 nc.sync.dma_start(
-                    out=y_scales[:, 4 * quad : 4 * quad + 4, m0 // 4 : m1 // 4].rearrange("g r w -> r g w"),
-                    in_=out_scales[32 * quad : 32 * quad + 4, :, m0:m1].bitcast(I32),
+                    out=y_scale_rows[:, 4 * quad : 4 * quad + 4, m0 // 4 : m1 // 4].rearrange("g r w -> r g w"),
+                    in_=y_scales[32 * quad : 32 * quad + 4, :, m0:m1].bitcast(I32),
                 )
 
-        tasks = {
-            "wt": w_turn, "we": w_empty, "wq": w_quantize, "xi": x_interleave, "xq": x_quantize, "mm": multiply,
-            "ge": gelu, "sc": scale, "tu": turn, "em": empty, "st": store_rows, "yi": y_interleave, "yq": y_quantize,
-            "yd": store_words, "sd": store_scales,
+
+        w_turn(0)
+        w_empty(0)
+        x_interleave(0)
+        x_interleave(2, hi=NARROW)
+        x_interleave(2, on_scalar, lo=NARROW)
+        w_quantize(0)
+        x_quantize(0)
+        x_quantize(2)
+        w_turn(1)
+        w_empty(1)
+        w_quantize(1)
+        w_turn(2)
+        x_interleave(1)
+        x_interleave(3, on_scalar, hi=NARROW)
+        x_interleave(3, lo=NARROW)
+        x_quantize(1)
+        x_quantize(3)
+        w_empty(2)
+        w_quantize(2)
+        w_turn(3)
+        w_empty(3)
+        w_quantize(3)
+        w_turn(4)
+        w_empty(4)
+        x_interleave(4)
+        w_quantize(4)
+        multiply(0)
+
+        gelu(0)
+        scale_on_scalar(0, 0)
+        w_turn(5)
+        w_turn(6)
+        w_empty(5)
+        w_empty(6)
+        multiply(2)
+        scale(0, 1, 2, 3)
+        x_quantize(4)
+        y_interleave(0)
+        x_interleave(5)
+
+        gelu(2)
+        w_turn(7)
+        w_empty(7)
+        turn(0, blocks(0))
+        empty(0, [0])
+        scale(2, 0)
+        w_quantize(5)
+        x_quantize(5)
+        scale(2, 1)
+        w_quantize(6)
+        scale(2, 2)
+        w_quantize(7)
+        scale(2, 3)
+        multiply(1)
+        x_interleave(6)
+        y_interleave(2)
+
+        gelu(1, [0, 1, 2])
+        empty(0, [1])
+        gelu(1, [3])
+        multiply(3)
+        turn(2, blocks(2))
+        scale(1, 0, 1)
+        x_interleave(7)
+        scale(1, 2, 3)
+        y_quantize(0)
+        y_quantize(2)
+        store_words(0)
+        store_rows(0, 0)
+        store_words(2)
+
+        gelu(3)
+        multiply(4)
+        empty(2, blocks(2))
+        turn(1, blocks(1))
+        scale(3, 0, 1)
+        x_quantize(6)
+        scale(3, 2, 3)
+        y_interleave(1)
+        x_interleave(8)
+        store_rows(2, 0)
+        store_rows(2, 1)
+
+        gelu(4)
+        multiply(5, [0])
+        turn(3, [0, 1])
+        empty(1, blocks(1))
+        multiply(5, [1])
+        turn(3, [2, 3])
+        multiply(5, [2, 3])
+        empty(3, blocks(3))
+        scale(4, 0, 1)
+        y_quantize(1)
+        x_quantize(7)
+        scale(4, 2, 3)
+        y_interleave(3)
+        store_rows(1, 0)
+        store_words(1)
+        store_rows(3, 0)
+        store_rows(3, 1)
+
+        vector_work = {
+            u: [(x_quantize, u + 3), (scale, u, 1, 2), (y_quantize, u - 2), (scale, u, 3), (x_interleave, u + 4),
+                (y_interleave, u - 1)]
+            for u in (5, 6, 7)
         }
-        for item in ORDER:
-            kind = item[:2]
-            args = [int(a) for a in item[2:].split(".")]
-            if kind in ("we", "em", "xi"):
-                on_vector = (kind == "xi") != (item in FLIPPED)
-                args.append(nc.vector.tensor_copy if on_vector else nc.scalar.copy)
-            tasks[kind](*args)
+        vector_work[5] = [(scale, 5, 0)] + vector_work[5]
+        vector_work[8] = [(x_interleave, 12), (x_quantize, 11), (scale, 8, 0, 1), (y_interleave, 7), (scale, 8, 2, 3),
+                          (y_quantize, 6)]
+        vector_work[9] = [(y_quantize, 7), (scale, 9, 0), (y_interleave, 8), (scale, 9, 1, 2, 3), (x_interleave, 13),
+                          (y_interleave, 9)]
+        vector_work[10] = [(y_quantize, 8), (y_quantize, 9), (scale, 10, 0, 1), (x_quantize, 12), (scale, 10, 2, 3),
+                           (x_quantize, 13), (y_interleave, 10)]
+        vector_work[11] = [(scale, 11, 0, 1), (y_quantize, 10), (scale, 11, 2, 3), (y_interleave, 11)]
+        vector_work[12] = [(empty, 11, [0], on_vector), (y_quantize, 11), (scale, 12, 0, 1, 2, 3),
+                           (empty, 11, [2], on_vector), (y_interleave, 12)]
+        vector_work[13] = [(scale, 13, 0, 1, 2, 3), (y_quantize, 12)]
+        vector_work[14] = [(y_interleave, 13), (y_quantize, 13), (empty, 13, [1], on_vector)]
+
+        stores = {u: [(store_words, u - 2), (store_rows, u - 1, 0), (store_rows, u - 1, 1)] for u in (5, 6, 7, 9)}
+        stores[8] = [(store_rows, 7, 0), (store_words, 6), (store_rows, 7, 1)]
+        stores[10] = [(store_words, 8), (store_scales, 0, 5), (store_rows, 9, 0), (store_words, 9), (store_rows, 9, 1)]
+        for u in (11, 12):
+            stores[u] = [(store_words, u - 1), (store_rows, u - 1, 0), (store_rows, u - 1, 1)]
+        stores[13] = [(store_rows, 12, 0), (store_words, 12), (store_rows, 12, 1)]
+        stores[14] = [(store_words, 13), (store_rows, 13, 0), (store_rows, 13, 1), (store_scales, 5, 7)]
+
+        for u in range(STEADY_FROM, UNITS + 1):
+            turn(u - 1, blocks(u - 1))
+            if u < UNITS:
+                gelu(u)
+            if u in SCALAR_SCALES:
+                scale_on_scalar(u, 0)
+            if u + 1 < UNITS:
+                multiply(u + 1)
+            empty(u - 1, [block for block in blocks(u - 1) if (u - 1, block) not in VECTOR_EMPTIES])
+            for step, *args in vector_work[u] + stores[u]:
+                step(*args)

from contextlib import ExitStack

import concourse.mybir as mybir
from concourse.masks import make_identity

B, S, C, H = 4, 1024, 768, 1024
M = B * C
FLOPS = 2 * H * S * M

F32 = mybir.dt.float32
BF16 = mybir.dt.bfloat16
I32 = mybir.dt.int32
U32 = mybir.dt.uint32
U8 = mybir.dt.uint8
FP8X4 = mybir.dt.float8_e4m3fn_x4
GELU = mybir.ActivationFunctionType.Gelu_apprx_tanh
COPY = mybir.ActivationFunctionType.Copy
MULT = mybir.AluOpType.mult

P = 128
PACK = 4
GROUP = P * PACK
PASSES = S // GROUP
H_GROUPS = H // GROUP

NARROW, WIDE = 256, 512
WIDTHS = [NARROW] + [WIDE] * 5 + [NARROW]
STARTS = [sum(WIDTHS[:n]) for n in range(len(WIDTHS) + 1)]
UNITS = len(WIDTHS) * H_GROUPS
UNIT_ORDER = [0, 2, 1] + list(range(3, UNITS))

SUM_BANKS, TURN_BANKS = 4, 4
W_GROUPED_BUFS, X_GROUPED_BUFS, Y_GROUPED_BUFS = 3, 3, 2
GELU_BUFS, SCALED_BUFS, ROWS_BUFS, Y_WORDS_BUFS = 8, 5, 5, 3

STEADY_FROM = 5
SCALAR_SCALES = (6, 7)
VECTOR_EMPTIES = ((11, 0), (11, 2), (13, 1))


def interleave(copy, grouped, rows):
    copy(
        out=grouped.rearrange("p (c i) t -> p c t i", i=4),
        in_=rows.rearrange("p t (c i) -> p c t i", i=4),
    )


def tile_token_mixing_hidden_planes_g1_kernel(tc, patches, w_mix, row_bias, row_scale, out_0, out_1, out_2):
    nc = tc.nc
    on_vector, on_scalar = nc.vector.tensor_copy, nc.scalar.copy
    y_rows = out_0.rearrange("b c h -> (b c) h")
    y_words = out_1.rearrange("g p m t -> g p (m t)").bitcast(I32)
    y_scale_rows = out_2.bitcast(I32)

    with ExitStack() as ctx:
        keep = ctx.enter_context(tc.tile_pool(name="keep", bufs=1))
        work = ctx.enter_context(tc.tile_pool(name="work", bufs=1))
        psum = ctx.enter_context(tc.psum_pool(name="psum", bufs=1))
        ctx.enter_context(tc.manual_schedule())

        ident = keep.tile([P, P], F32, name="ident")
        make_identity(nc, ident[:])
        warm = keep.tile([P, 1], F32, name="warm")
        nc.scalar.activation(out=warm[:], in_=ident[:, 0:1], func=GELU)

        w_raw, x_raw = {}, {}

        def load_w(q):
            g, t = divmod(q, PACK)
            rows = w_mix[g * GROUP : (g + 1) * GROUP, :].rearrange("(p t) k -> p t k", t=PACK)
            w_raw[q] = keep.tile([P, S], BF16, name="w_raw%d" % q)
            nc.sync.dma_start(out=w_raw[q][:], in_=rows[:, t, :])

        def load_x(b, j):
            rows = patches[b, j * GROUP : (j + 1) * GROUP, :].rearrange("(p t) c -> p t c", t=PACK)
            x_raw[b, j] = keep.tile([P, PACK, C], BF16, name="x_raw%d_%d" % (b, j))
            nc.sync.dma_start(out=x_raw[b, j][:], in_=rows)

        def load_per_row(vec, name):
            narrow = keep.tile([P, H_GROUPS, PACK], BF16, name=name + "_bf16")
            wide = keep.tile([P, H_GROUPS, PACK], F32, name=name)
            nc.sync.dma_start(out=narrow[:], in_=vec.rearrange("(g p t) -> p g t", p=P, t=PACK))
            nc.gpsimd.tensor_copy(out=wide[:], in_=narrow[:])
            return wide

        load_w(0)
        load_x(0, 0)
        load_w(1)
        load_w(2)
        bias = load_per_row(row_bias, "bias")
        gain = load_per_row(row_scale, "gain")
        load_x(0, 1)
        load_w(3)
        load_w(4)
        load_x(1, 0)
        load_w(5)
        load_w(6)
        load_x(1, 1)
        load_w(7)
        for b in range(2, B):
            for j in range(PASSES):
                load_x(b, j)

        banks_taken = {"sums": 0, "turn": 0}

        def psum_bank(kind, depth, shape):
            tag = "%s%d" % (kind, banks_taken[kind] % depth)
            banks_taken[kind] += 1
            return psum.tile(shape, F32, name=kind, tag=tag)

        w_turned, w_grouped, w_codes, w_scales = {}, {}, {}, {}

        def w_turn(q):
            pairs = w_raw[q][:].bitcast(F32)
            w_turned[q] = psum_bank("turn", TURN_BANKS, [P, PASSES, 2, P])
            for j in range(PASSES):
                for u in range(2):
                    nc.tensor.transpose(
                        w_turned[q][:, j, u, :], pairs[:, 2 * P * j + u : 2 * P * (j + 1) : 2], ident[:]
                    )

        def w_empty(q):
            w_grouped[q] = work.tile(
                [P, PASSES, P, 2], F32, name="w_grouped", tag="w_grouped%d" % (q % W_GROUPED_BUFS), align_bytes=64
            )
            on_scalar(out=w_grouped[q][:], in_=w_turned[q][:].rearrange("p j u r -> p j r u"))

        def w_quantize(q):
            w_codes[q] = keep.tile([P, PASSES, P], U32, name="w_codes%d" % q, align_bytes=64)
            w_scales[q] = keep.tile([P, PASSES, P], U8, name="w_scales%d" % q, align_bytes=64)
            nc.vector.quantize_mx(
                out=w_codes[q][:].rearrange("p j r -> p (j r)").bitcast(FP8X4),
                scales=w_scales[q][:].rearrange("p j r -> p (j r)"),
                in_=w_grouped[q][:].rearrange("p j r u -> p (j r u)").bitcast(BF16),
            )

        x_grouped, x_codes, x_scales = {}, {}, {}
        wide_x = [x for x in range(UNITS) if WIDTHS[x // PASSES] == WIDE]

        def x_interleave(x, copy=on_vector, lo=0, hi=WIDE):
            n, j = divmod(x, PASSES)
            if x not in x_grouped:
                tag = "x_grouped%d" % (wide_x.index(x) % X_GROUPED_BUFS) if x in wide_x else "x_narrow%d" % x
                x_grouped[x] = work.tile([P, WIDTHS[n], PACK], BF16, name="x_grouped", tag=tag, align_bytes=64)
            for b in range(B):
                m0 = max(STARTS[n] + lo, b * C)
                m1 = min(STARTS[n] + hi, STARTS[n + 1], (b + 1) * C)
                if m0 < m1:
                    interleave(
                        copy,
                        x_grouped[x][:, m0 - STARTS[n] : m1 - STARTS[n], :],
                        x_raw[b, j][:, :, m0 - b * C : m1 - b * C],
                    )

        def x_quantize(x):
            width = WIDTHS[x // PASSES]
            x_codes[x] = keep.tile([P, width], U32, name="x_codes%d" % x, align_bytes=64)
            x_scales[x] = keep.tile([P, width], U8, name="x_scales%d" % x, align_bytes=64)
            nc.vector.quantize_mx(
                out=x_codes[x][:].bitcast(FP8X4),
                scales=x_scales[x][:],
                in_=x_grouped[x][:].rearrange("p m t -> p (m t)"),
            )

        sums, gelus, scaled = {}, {}, {}

        def multiply(unit, slices=range(PACK)):
            n, g = divmod(unit, H_GROUPS)
            for t in slices:
                q = PACK * g + t
                sums[unit, t] = psum_bank("sums", SUM_BANKS, [P, WIDTHS[n]])
                for j in range(PASSES):
                    x = PASSES * n + j
                    nc.tensor.matmul_mx(
                        out=sums[unit, t][:],
                        lhsT=w_codes[q][:, j, :].bitcast(FP8X4),
                        lhsT_scale=w_scales[q][:, j, :],
                        rhs=x_codes[x][:].bitcast(FP8X4),
                        rhs_scale=x_scales[x][:],
                        start=(j == 0),
                        stop=(j == PASSES - 1),
                    )

        def gelu(unit, slices=range(PACK)):
            n, g = divmod(unit, H_GROUPS)
            for t in slices:
                tag = "gelu%d" % ((PACK * UNIT_ORDER.index(unit) + t) % GELU_BUFS)
                gelus[unit, t] = work.tile([P, WIDTHS[n]], F32, name="gelu", tag=tag)
                nc.scalar.activation(
                    out=gelus[unit, t][:], in_=sums[unit, t][:], func=GELU, bias=bias[:, g, t : t + 1]
                )

        def scaled_tile(unit):
            if unit not in scaled:
                tag = "scaled%d" % (UNIT_ORDER.index(unit) % SCALED_BUFS)
                scaled[unit] = work.tile([P, PACK, WIDTHS[unit // H_GROUPS]], F32, name="scaled", tag=tag)
            return scaled[unit]

        def scale(unit, *slices):
            for t in slices:
                nc.vector.tensor_scalar(
                    out=scaled_tile(unit)[:, t, :],
                    in0=gelus[unit, t][:],
                    scalar1=gain[:, unit % H_GROUPS, t : t + 1],
                    scalar2=None,
                    op0=MULT,
                )

        def scale_on_scalar(unit, t):
            nc.scalar.activation(
                out=scaled_tile(unit)[:, t, :],
                in_=gelus[unit, t][:],
                func=COPY,
                scale=gain[:, unit % H_GROUPS, t : t + 1],
            )

        turned, rows_out = {}, {}

        def blocks(unit):
            return range(WIDTHS[unit // H_GROUPS] // P)

        def blocks_per_store(unit):
            return 1 if unit >= UNITS - H_GROUPS else 2

        row_stores = [(u, k) for u in UNIT_ORDER for k in range(len(blocks(u)) // blocks_per_store(u))]

        def turn(unit, which):
            for block in which:
                turned[unit, block] = psum_bank("turn", TURN_BANKS, [P, PACK, P])
                for t in range(PACK):
                    nc.tensor.transpose(
                        turned[unit, block][:, t, :], scaled[unit][:, t, block * P : (block + 1) * P], ident[:]
                    )

        def empty(unit, which, copy=on_scalar):
            per = blocks_per_store(unit)
            for block in which:
                key = (unit, block // per)
                if key not in rows_out:
                    tag = "rows_out%d" % (row_stores.index(key) % ROWS_BUFS)
                    rows_out[key] = work.tile([P, per, P, PACK], F32, name="rows_out", tag=tag)
                copy(out=rows_out[key][:, block % per], in_=turned[unit, block][:].rearrange("m t p -> m p t"))

        def store_rows(unit, k):
            n, g = divmod(unit, H_GROUPS)
            rows = blocks_per_store(unit) * P
            m0 = STARTS[n] + rows * k
            nc.sync.dma_start(
                out=y_rows[m0 : m0 + rows, g * GROUP : (g + 1) * GROUP].rearrange("(a m) h -> m a h", m=P),
                in_=rows_out[unit, k][:].rearrange("m a p t -> m a (p t)"),
            )

        y_grouped, y_codes = {}, {}
        y_scales = keep.tile([P, H_GROUPS, M], U8, name="y_scales", align_bytes=64)

        def y_interleave(unit):
            tag = "y_grouped%d" % (UNIT_ORDER.index(unit) % Y_GROUPED_BUFS)
            y_grouped[unit] = work.tile(
                [P, WIDTHS[unit // H_GROUPS], PACK], BF16, name="y_grouped", tag=tag, align_bytes=64
            )
            interleave(on_vector, y_grouped[unit][:], scaled[unit][:])

        def y_quantize(unit):
            n, g = divmod(unit, H_GROUPS)
            tag = "y_codes%d" % (UNIT_ORDER.index(unit) % Y_WORDS_BUFS)
            y_codes[unit] = work.tile([P, WIDTHS[n]], U32, name="y_codes", tag=tag, align_bytes=64)
            nc.vector.quantize_mx(
                out=y_codes[unit][:].bitcast(FP8X4),
                scales=y_scales[:, g, STARTS[n] : STARTS[n + 1]],
                in_=y_grouped[unit][:].rearrange("p m t -> p (m t)"),
            )

        def store_words(unit):
            n, g = divmod(unit, H_GROUPS)
            nc.sync.dma_start(out=y_words[g, :, STARTS[n] : STARTS[n + 1]], in_=y_codes[unit][:].bitcast(I32))

        def store_scales(first_chunk, end_chunk):
            m0, m1 = STARTS[first_chunk], STARTS[end_chunk]
            for quad in range(4):
                nc.sync.dma_start(
                    out=y_scale_rows[:, 4 * quad : 4 * quad + 4, m0 // 4 : m1 // 4].rearrange("g r w -> r g w"),
                    in_=y_scales[32 * quad : 32 * quad + 4, :, m0:m1].bitcast(I32),
                )


        w_turn(0)
        w_empty(0)
        x_interleave(0)
        x_interleave(2, hi=NARROW)
        x_interleave(2, on_scalar, lo=NARROW)
        w_quantize(0)
        x_quantize(0)
        x_quantize(2)
        w_turn(1)
        w_empty(1)
        w_quantize(1)
        w_turn(2)
        x_interleave(1)
        x_interleave(3, on_scalar, hi=NARROW)
        x_interleave(3, lo=NARROW)
        x_quantize(1)
        x_quantize(3)
        w_empty(2)
        w_quantize(2)
        w_turn(3)
        w_empty(3)
        w_quantize(3)
        w_turn(4)
        w_empty(4)
        x_interleave(4)
        w_quantize(4)
        multiply(0)

        gelu(0)
        scale_on_scalar(0, 0)
        w_turn(5)
        w_turn(6)
        w_empty(5)
        w_empty(6)
        multiply(2)
        scale(0, 1, 2, 3)
        x_quantize(4)
        y_interleave(0)
        x_interleave(5)

        gelu(2)
        w_turn(7)
        w_empty(7)
        turn(0, blocks(0))
        empty(0, [0])
        scale(2, 0)
        w_quantize(5)
        x_quantize(5)
        scale(2, 1)
        w_quantize(6)
        scale(2, 2)
        w_quantize(7)
        scale(2, 3)
        multiply(1)
        x_interleave(6)
        y_interleave(2)

        gelu(1, [0, 1, 2])
        empty(0, [1])
        gelu(1, [3])
        multiply(3)
        turn(2, blocks(2))
        scale(1, 0, 1)
        x_interleave(7)
        scale(1, 2, 3)
        y_quantize(0)
        y_quantize(2)
        store_words(0)
        store_rows(0, 0)
        store_words(2)

        gelu(3)
        multiply(4)
        empty(2, blocks(2))
        turn(1, blocks(1))
        scale(3, 0, 1)
        x_quantize(6)
        scale(3, 2, 3)
        y_interleave(1)
        x_interleave(8)
        store_rows(2, 0)
        store_rows(2, 1)

        gelu(4)
        multiply(5, [0])
        turn(3, [0, 1])
        empty(1, blocks(1))
        multiply(5, [1])
        turn(3, [2, 3])
        multiply(5, [2, 3])
        empty(3, blocks(3))
        scale(4, 0, 1)
        y_quantize(1)
        x_quantize(7)
        scale(4, 2, 3)
        y_interleave(3)
        store_rows(1, 0)
        store_words(1)
        store_rows(3, 0)
        store_rows(3, 1)

        vector_work = {
            u: [(x_quantize, u + 3), (scale, u, 1, 2), (y_quantize, u - 2), (scale, u, 3), (x_interleave, u + 4),
                (y_interleave, u - 1)]
            for u in (5, 6, 7)
        }
        vector_work[5] = [(scale, 5, 0)] + vector_work[5]
        vector_work[8] = [(x_interleave, 12), (x_quantize, 11), (scale, 8, 0, 1), (y_interleave, 7), (scale, 8, 2, 3),
                          (y_quantize, 6)]
        vector_work[9] = [(y_quantize, 7), (scale, 9, 0), (y_interleave, 8), (scale, 9, 1, 2, 3), (x_interleave, 13),
                          (y_interleave, 9)]
        vector_work[10] = [(y_quantize, 8), (y_quantize, 9), (scale, 10, 0, 1), (x_quantize, 12), (scale, 10, 2, 3),
                           (x_quantize, 13), (y_interleave, 10)]
        vector_work[11] = [(scale, 11, 0, 1), (y_quantize, 10), (scale, 11, 2, 3), (y_interleave, 11)]
        vector_work[12] = [(empty, 11, [0], on_vector), (y_quantize, 11), (scale, 12, 0, 1, 2, 3),
                           (empty, 11, [2], on_vector), (y_interleave, 12)]
        vector_work[13] = [(scale, 13, 0, 1, 2, 3), (y_quantize, 12)]
        vector_work[14] = [(y_interleave, 13), (y_quantize, 13), (empty, 13, [1], on_vector)]

        stores = {u: [(store_words, u - 2), (store_rows, u - 1, 0), (store_rows, u - 1, 1)] for u in (5, 6, 7, 9)}
        stores[8] = [(store_rows, 7, 0), (store_words, 6), (store_rows, 7, 1)]
        stores[10] = [(store_words, 8), (store_scales, 0, 5), (store_rows, 9, 0), (store_words, 9), (store_rows, 9, 1)]
        for u in (11, 12):
            stores[u] = [(store_words, u - 1), (store_rows, u - 1, 0), (store_rows, u - 1, 1)]
        stores[13] = [(store_rows, 12, 0), (store_words, 12), (store_rows, 12, 1)]
        stores[14] = [(store_words, 13), (store_rows, 13, 0), (store_rows, 13, 1), (store_scales, 5, 7)]

        for u in range(STEADY_FROM, UNITS + 1):
            turn(u - 1, blocks(u - 1))
            if u < UNITS:
                gelu(u)
            if u in SCALAR_SCALES:
                scale_on_scalar(u, 0)
            if u + 1 < UNITS:
                multiply(u + 1)
            empty(u - 1, [block for block in blocks(u - 1) if (u - 1, block) not in VECTOR_EMPTIES])
            for step, *args in vector_work[u] + stores[u]:
                step(*args)
